import numpy as np
import ml_dtypes


def mxq(x, axis, fmt="e4m3"):
    dtype, down = {"e4m3": (ml_dtypes.float8_e4m3fn, 7), "e5m2": (ml_dtypes.float8_e5m2, 14)}[fmt]
    v = np.moveaxis(np.asarray(x, np.float32).astype(ml_dtypes.bfloat16).astype(np.float64), axis, -1)
    blocks = v.reshape(v.shape[:-1] + (-1, 32))
    amax = np.abs(blocks).max(-1, keepdims=True)
    byte = np.maximum(np.where(amax > 0, np.frexp(amax)[1] - 1 + 127, 0) - down, 1)
    scale = np.exp2(byte - 127.0)
    codes = (blocks / scale).astype(np.float32).astype(dtype).astype(np.float64)
    return np.moveaxis((codes * scale).reshape(v.shape), -1, axis)


WIDE = False


def mx_kscale(k):
    if not WIDE:
        return np.ones(k)
    levels = np.array([10, -10, 5, -5, 0])
    if k % 512:
        return np.exp2(np.random.permutation(np.resize(levels, k // 32))).repeat(32)
    a = np.empty((k // 512, 16))
    for p in range(k // 512):
        a[p, :8] = np.random.permutation(np.resize(levels, 8))
        for g in range(8):
            far = levels[np.abs(levels - a[p, g]) >= 10]
            a[p, g + 8] = far[np.random.randint(len(far))]
    return np.exp2(a.ravel()).repeat(32)


def f64(x):
    return np.asarray(x).astype(np.float64)


def striped(idx):
    return np.tile(np.asarray(idx).reshape(-1, 16).T, (8, 1)).astype(np.uint16)


def unstriped(offs):
    return offs[:16].T.reshape(-1).astype(np.int64)


E2M1 = np.array([0.0, 0.5, 1.0, 1.5, 2.0, 3.0, 4.0, 6.0, -0.0, -0.5, -1.0, -1.5, -2.0, -3.0, -4.0, -6.0])


def pack_weight(w, fmt):
    k, n = w.shape
    w = f64(np.asarray(w, np.float32).astype(ml_dtypes.bfloat16)).reshape(k // 32, 32, n)
    amax = np.abs(w).max(1)
    if fmt == "e4m3":
        byte = np.frexp(amax)[1] - 1 + 127 - 7
    else:
        mant, ex = np.frexp(amax / 6.0)
        byte = np.where(mant > 0.5, ex, ex - 1) + 127
    byte = np.clip(np.where(amax > 0, byte, 1), 1, 254)
    scaled = (w * np.exp2(127.0 - byte)[:, None, :]).reshape(k, n).astype(np.float32)
    by_word = np.ascontiguousarray(scaled.reshape(k // 512, 128, 4, n).transpose(0, 1, 3, 2))
    if fmt == "e4m3":
        words = by_word.astype(ml_dtypes.float8_e4m3fn).view(np.uint8)
    else:
        c = by_word.astype(ml_dtypes.float4_e2m1fn).view(np.uint8) & 0xF
        words = (c[..., 0::2] | (c[..., 1::2] << 4)).reshape(k // 512, 128, 2 * n)
    return np.ascontiguousarray(words), np.ascontiguousarray(byte.astype(np.uint8).reshape(k // 512, 16, n))


def unpack_weight(words, scales, fmt):
    g, _, n = scales.shape
    words = np.ascontiguousarray(words).reshape(g, 128, n, -1)
    if fmt == "e4m3":
        vals = words.view(ml_dtypes.float8_e4m3fn).astype(np.float64)
    else:
        nib = np.empty((g, 128, n, 4), np.uint8)
        nib[..., 0::2] = words & 0xF
        nib[..., 1::2] = words >> 4
        vals = E2M1[nib]
    vals = vals * np.repeat(np.exp2(scales.astype(np.float64) - 127.0), 8, axis=1)[..., None]
    return vals.transpose(0, 1, 3, 2).reshape(g * 512, n)


def softplus(v):
    return np.log(1.0 + np.exp(v))


D, T, V, I, Q = 512, 2048, 1024, 512, 128


def setup_inputs():
    n = np.random.standard_normal
    idx = np.random.permutation(T)[:V]
    idx2 = np.random.randint(0, V, I)
    idx3 = np.random.randint(0, V, I)
    idx4 = np.random.randint(0, V, I)
    fd = mx_kscale(D)
    nodesp = pack_weight(n((D, T)) / fd[:, None], "e2m1")
    return {
        "hid": (n((D, Q)) * 1.5 / np.sqrt(D) * fd[:, None]).astype(np.float32),
        "nodes_words": nodesp[0],
        "nodes_scales": nodesp[1],
        "s1": (np.random.uniform(-1.5, 1.5, (1, I))).astype(np.float32),
        "s2": (np.random.uniform(-1.5, 1.5, (1, I))).astype(np.float32),
        "s3": (np.random.uniform(-1.5, 1.5, (1, I))).astype(np.float32),
        "offs": striped(idx),
        "offs2": striped(idx2),
        "offs3": striped(idx3),
        "offs4": striped(idx4),
    }


def reference(hid, nodes_words, nodes_scales, s1, s2, s3, offs, offs2, offs3, offs4):
    idx = unstriped(offs)
    idx2 = unstriped(offs2)
    idx3 = unstriped(offs3)
    idx4 = unstriped(offs4)
    nodesu = unpack_weight(nodes_words, nodes_scales, "e2m1")
    hidq = mxq(f64(hid), 0, "e4m3")
    nodesidxg = nodesu[:, idx]
    a = hidq.T @ nodesidxg
    y = (softplus(a[:, idx2] * f64(s1)) + softplus(a[:, idx3] * f64(s2)) + softplus(a[:, idx4] * f64(s3))) * (-1.0)
    return y

@@ -1,0 +1,126 @@
+from contextlib import ExitStack
+
+import concourse.mybir as mybir
+
+D, T, V, I, Q = 512, 2048, 1024, 512, 128
+FLOPS = 2 * D * Q * V
+
+F32 = mybir.dt.float32
+BF16 = mybir.dt.bfloat16
+I32 = mybir.dt.int32
+U32 = mybir.dt.uint32
+U16 = mybir.dt.uint16
+U8 = mybir.dt.uint8
+FP8X4 = mybir.dt.float8_e4m3fn_x4
+FP4X4 = mybir.dt.float4_e2m1fn_x4
+ALU = mybir.AluOpType
+ACT = mybir.ActivationFunctionType
+
+P = 128
+PACK = 4
+GROUP = 16
+
+
+def entries(offsets, lo, hi):
+    return offsets[:, lo // GROUP : hi // GROUP]
+
+
+def tile_attend_codepaths_kernel(tc, hid, nodes_words, nodes_scales, s1, s2, s3, offs, offs2, offs3, offs4, out):
+    nc = tc.nc
+    with ExitStack() as ctx:
+        lists = ctx.enter_context(tc.tile_pool(name="lists", bufs=1))
+        sb = ctx.enter_context(tc.tile_pool(name="sb", bufs=1))
+        psum = ctx.enter_context(tc.psum_pool(name="psum", bufs=1))
+
+        warm_in = sb.tile([P, 1], F32)
+        warm_out = sb.tile([P, 1], F32)
+        store_scales = sb.tile([P, T], U8, align_bytes=64)
+        nc.vector.memset(store_scales[:].bitcast(I32), 0)
+        nc.vector.memset(warm_in[:], 0.0)
+        nc.scalar.activation(warm_out[:], warm_in[:], ACT.Sigmoid)
+
+        store_words = sb.tile([P, T], U16, align_bytes=64)
+        nc.sync.dma_start(store_words[:].bitcast(I32), nodes_words[0].bitcast(I32))
+        node_list = lists.tile([P, V // GROUP], U16)
+        nc.sync.dma_start(node_list[:], offs)
+        hid_raw = sb.tile([P, PACK, Q], F32)
+        nc.sync.dma_start(hid_raw[:], hid.rearrange("(p t) q -> p t q", t=PACK))
+        for quad in range(4):
+            nc.sync.dma_start(
+                store_scales[32 * quad : 32 * quad + 4, :].bitcast(I32),
+                nodes_scales[0, 4 * quad : 4 * quad + 4, :].bitcast(I32),
+            )
+        path_lists = []
+        turns = []
+        for j, (offs_j, s_j) in enumerate(((offs2, s1), (offs3, s2), (offs4, s3))):
+            path_list = lists.tile([P, I // GROUP], U16, name="path_list%d" % j)
+            nc.sync.dma_start(path_list[:], offs_j)
+            turn = sb.tile([P, I], F32, name="turn%d" % j)
+            nc.sync.dma_start(turn[:], s_j[0].partition_broadcast(P))
+            path_lists.append(path_list)
+            turns.append(turn)
+
+        hid_bf = sb.tile([P, Q, PACK], BF16, align_bytes=64, tag="staging")
+        nc.scalar.copy(hid_bf[:], hid_raw[:].rearrange("p t q -> p q t"))
+        hid_codes = sb.tile([P, Q], U32, align_bytes=64)
+        hid_scales = sb.tile([P, Q], U8, align_bytes=64)
+
+        words = sb.tile([P, V], U16, align_bytes=64)
+        for lo, hi in ((0, 512), (512, 1024)):
+            nc.vector.tensor_copy(words[:, lo:hi], store_words[:].indirect(entries(node_list, lo, hi)))
+        nc.vector.quantize_mx(
+            out=hid_codes[:].bitcast(FP8X4), scales=hid_scales[:], in_=hid_bf[:].rearrange("p q t -> p (q t)")
+        )
+        score = sb.tile([P, V], F32)
+        scales_a = sb.tile([P, 512], U8, align_bytes=64)
+        scales_b = sb.tile([P, 512], U8, align_bytes=64, tag="staging")
+        for lo, hi, pieces in ((0, 512, 1), (512, 768, 1), (768, 1024, 2)):
+            scales = scales_a if lo < 512 else scales_b
+            base = 0 if lo < 512 else 512
+            nc.vector.tensor_copy(scales[:, lo - base : hi - base], store_scales[:].indirect(entries(node_list, lo, hi)))
+            width = (hi - lo) // pieces
+            for piece in range(pieces):
+                cols = slice(lo + piece * width, lo + (piece + 1) * width)
+                bank = psum.tile([P, width], F32, name="bank%d" % cols.start)
+                nc.tensor.matmul_mx(
+                    out=bank[:],
+                    lhsT=hid_codes[:].bitcast(FP8X4),
+                    lhsT_scale=hid_scales[:],
+                    rhs=words[:, cols].bitcast(FP4X4),
+                    rhs_scale=scales[:, cols.start - base : cols.stop - base],
+                    start=True,
+                    stop=True,
+                )
+                if piece == 0:
+                    nc.scalar.copy(score[:, cols], bank[:])
+                else:
+                    nc.vector.tensor_copy(score[:, cols], bank[:])
+
+        halves = ((0, 256), (256, 512))
+        x = [sb.tile([P, I], F32, name="x%d" % j) for j in range(3)]
+        mag = [sb.tile([P, I], F32, name="mag%d" % j) for j in range(3)]
+        sig = [sb.tile([P, I], F32, name="sig%d" % j) for j in range(3)]
+        for j in range(3):
+            for lo, hi in halves:
+                nc.vector.tensor_tensor(
+                    x[j][:, lo:hi], score[:].indirect(entries(path_lists[j], lo, hi)), turns[j][:, lo:hi], ALU.mult
+                )
+                nc.scalar.activation(mag[j][:, lo:hi], x[j][:, lo:hi], ACT.Abs)
+                nc.scalar.activation(sig[j][:, lo:hi], mag[j][:, lo:hi], ACT.Sigmoid)
+
+        prod2 = sb.tile([P, I], F32)
+        prod3 = sb.tile([P, I], F32)
+        pos1 = sb.tile([P, I], F32)
+        pos2 = sb.tile([P, I], F32)
+        pos3 = sb.tile([P, I], F32)
+        logp = sb.tile([P, I], F32)
+        res = sb.tile([P, I], F32)
+        nc.vector.tensor_scalar(pos1[:], x[0][:], 0.0, None, ALU.max)
+        nc.vector.tensor_tensor(prod2[:], sig[0][:], sig[1][:], ALU.mult)
+        nc.vector.scalar_tensor_tensor(pos2[:], x[1][:], 0.0, pos1[:], ALU.max, ALU.add)
+        nc.vector.tensor_tensor(prod3[:], prod2[:], sig[2][:], ALU.mult)
+        nc.vector.scalar_tensor_tensor(pos3[:], x[2][:], 0.0, pos2[:], ALU.max, ALU.add)
+        for lo, hi in halves:
+            nc.scalar.activation(logp[:, lo:hi], prod3[:, lo:hi], ACT.Ln)
+            nc.vector.tensor_tensor(res[:, lo:hi], logp[:, lo:hi], pos3[:, lo:hi], ALU.subtract)
+            nc.sync.dma_start(out[:, lo:hi], res[:, lo:hi])

@@ -43,7 +43,7 @@ def tile_attend_codepaths_kernel(tc, hid, nodes_words, nodes_scales, s1, s2, s3,
         nc.sync.dma_start(store_words[:].bitcast(I32), nodes_words[0].bitcast(I32))
         node_list = lists.tile([P, V // GROUP], U16)
         nc.sync.dma_start(node_list[:], offs)
-        hid_raw = sb.tile([P, PACK, Q], F32)
+        hid_raw = sb.tile([P, PACK, Q], F32, tag="rows")
         nc.sync.dma_start(hid_raw[:], hid.rearrange("(p t) q -> p t q", t=PACK))
         for quad in range(4):
             nc.sync.dma_start(
@@ -51,17 +51,16 @@ def tile_attend_codepaths_kernel(tc, hid, nodes_words, nodes_scales, s1, s2, s3,
                 nodes_scales[0, 4 * quad : 4 * quad + 4, :].bitcast(I32),
             )
         path_lists = []
-        turns = []
-        for j, (offs_j, s_j) in enumerate(((offs2, s1), (offs3, s2), (offs4, s3))):
+        for j, offs_j in enumerate((offs2, offs3, offs4)):
             path_list = lists.tile([P, I // GROUP], U16, name="path_list%d" % j)
             nc.sync.dma_start(path_list[:], offs_j)
-            turn = sb.tile([P, I], F32, name="turn%d" % j)
-            nc.sync.dma_start(turn[:], s_j[0].partition_broadcast(P))
             path_lists.append(path_list)
-            turns.append(turn)
 
         hid_bf = sb.tile([P, Q, PACK], BF16, align_bytes=64, tag="staging")
         nc.scalar.copy(hid_bf[:], hid_raw[:].rearrange("p t q -> p q t"))
+        turns = sb.tile([P, 3 * I], F32, tag="rows")
+        for j, s_j in enumerate((s1, s2, s3)):
+            nc.sync.dma_start(turns[:, j * I : (j + 1) * I], s_j[0].partition_broadcast(P))
         hid_codes = sb.tile([P, Q], U32, align_bytes=64)
         hid_scales = sb.tile([P, Q], U8, align_bytes=64)
 
@@ -71,7 +70,7 @@ def tile_attend_codepaths_kernel(tc, hid, nodes_words, nodes_scales, s1, s2, s3,
         nc.vector.quantize_mx(
             out=hid_codes[:].bitcast(FP8X4), scales=hid_scales[:], in_=hid_bf[:].rearrange("p q t -> p (q t)")
         )
-        score = sb.tile([P, V], F32)
+        score = sb.tile([P, V], F32, tag="scores")
         scales_a = sb.tile([P, 512], U8, align_bytes=64)
         scales_b = sb.tile([P, 512], U8, align_bytes=64, tag="staging")
         for lo, hi, pieces in ((0, 512, 1), (512, 768, 1), (768, 1024, 2)):
@@ -96,31 +95,36 @@ def tile_attend_codepaths_kernel(tc, hid, nodes_words, nodes_scales, s1, s2, s3,
                 else:
                     nc.vector.tensor_copy(score[:, cols], bank[:])
 
-        halves = ((0, 256), (256, 512))
         x = [sb.tile([P, I], F32, name="x%d" % j) for j in range(3)]
         mag = [sb.tile([P, I], F32, name="mag%d" % j) for j in range(3)]
         sig = [sb.tile([P, I], F32, name="sig%d" % j) for j in range(3)]
-        for j in range(3):
-            for lo, hi in halves:
-                nc.vector.tensor_tensor(
-                    x[j][:, lo:hi], score[:].indirect(entries(path_lists[j], lo, hi)), turns[j][:, lo:hi], ALU.mult
-                )
-                nc.scalar.activation(mag[j][:, lo:hi], x[j][:, lo:hi], ACT.Abs)
-                nc.scalar.activation(sig[j][:, lo:hi], mag[j][:, lo:hi], ACT.Sigmoid)
+        pieces = [(j, lo, lo + w) for j, w in enumerate((256, 256, 128)) for lo in range(0, I, w)]
+        waiting = None
+        for j, lo, hi in pieces:
+            nc.vector.tensor_tensor(
+                x[j][:, lo:hi], score[:].indirect(entries(path_lists[j], lo, hi)), turns[:, j * I + lo : j * I + hi], ALU.mult
+            )
+            nc.scalar.activation(mag[j][:, lo:hi], x[j][:, lo:hi], ACT.Abs)
+            if waiting is not None:
+                nc.scalar.activation(waiting[0], waiting[1], ACT.Sigmoid)
+            waiting = (sig[j][:, lo:hi], mag[j][:, lo:hi])
+        nc.scalar.activation(waiting[0], waiting[1], ACT.Sigmoid)
 
-        prod2 = sb.tile([P, I], F32)
+        prod2 = sb.tile([P, I], F32, tag="rows")
         prod3 = sb.tile([P, I], F32)
-        pos1 = sb.tile([P, I], F32)
+        pos1 = sb.tile([P, I], F32, tag="scores")
         pos2 = sb.tile([P, I], F32)
         pos3 = sb.tile([P, I], F32)
         logp = sb.tile([P, I], F32)
         res = sb.tile([P, I], F32)
-        nc.vector.tensor_scalar(pos1[:], x[0][:], 0.0, None, ALU.max)
         nc.vector.tensor_tensor(prod2[:], sig[0][:], sig[1][:], ALU.mult)
-        nc.vector.scalar_tensor_tensor(pos2[:], x[1][:], 0.0, pos1[:], ALU.max, ALU.add)
+        nc.vector.tensor_scalar(pos1[:], x[0][:], 0.0, None, ALU.max)
         nc.vector.tensor_tensor(prod3[:], prod2[:], sig[2][:], ALU.mult)
+        nc.vector.scalar_tensor_tensor(pos2[:], x[1][:], 0.0, pos1[:], ALU.max, ALU.add)
         nc.vector.scalar_tensor_tensor(pos3[:], x[2][:], 0.0, pos2[:], ALU.max, ALU.add)
-        for lo, hi in halves:
+        for lo in range(0, I, 128):
+            hi = lo + 128
             nc.scalar.activation(logp[:, lo:hi], prod3[:, lo:hi], ACT.Ln)
             nc.vector.tensor_tensor(res[:, lo:hi], logp[:, lo:hi], pos3[:, lo:hi], ALU.subtract)
-            nc.sync.dma_start(out[:, lo:hi], res[:, lo:hi])
+            if hi % 256 == 0:
+                nc.sync.dma_start(out[:, hi - 256 : hi], res[:, hi - 256 : hi])

@@ -117,11 +117,15 @@ def tile_attend_codepaths_kernel(tc, hid, nodes_words, nodes_scales, s1, s2, s3,
         pos3 = sb.tile([P, I], F32)
         logp = sb.tile([P, I], F32)
         res = sb.tile([P, I], F32)
-        nc.vector.tensor_tensor(prod2[:], sig[0][:], sig[1][:], ALU.mult)
         nc.vector.tensor_scalar(pos1[:], x[0][:], 0.0, None, ALU.max)
-        nc.vector.tensor_tensor(prod3[:], prod2[:], sig[2][:], ALU.mult)
+        nc.vector.tensor_tensor(prod2[:], sig[0][:], sig[1][:], ALU.mult)
         nc.vector.scalar_tensor_tensor(pos2[:], x[1][:], 0.0, pos1[:], ALU.max, ALU.add)
-        nc.vector.scalar_tensor_tensor(pos3[:], x[2][:], 0.0, pos2[:], ALU.max, ALU.add)
+        for lo in range(0, I, 256):
+            cols = slice(lo, lo + 256)
+            nc.vector.tensor_tensor(prod3[:, cols], prod2[:, cols], sig[2][:, cols], ALU.mult)
+        for lo in range(0, I, 256):
+            cols = slice(lo, lo + 256)
+            nc.vector.scalar_tensor_tensor(pos3[:, cols], x[2][:, cols], 0.0, pos2[:, cols], ALU.max, ALU.add)
         for lo in range(0, I, 128):
             hi = lo + 128
             nc.scalar.activation(logp[:, lo:hi], prod3[:, lo:hi], ACT.Ln)

@@ -35,7 +35,9 @@ def tile_attend_codepaths_kernel(tc, hid, nodes_words, nodes_scales, s1, s2, s3,
         warm_in = sb.tile([P, 1], F32)
         warm_out = sb.tile([P, 1], F32)
         store_scales = sb.tile([P, T], U8, align_bytes=64)
-        nc.vector.memset(store_scales[:].bitcast(I32), 0)
+        zero_view = store_scales[:].bitcast(I32)
+        nc.vector.memset(zero_view[:, : T // 8], 0)
+        nc.gpsimd.memset(zero_view[:, T // 8 :], 0)
         nc.vector.memset(warm_in[:], 0.0)
         nc.scalar.activation(warm_out[:], warm_in[:], ACT.Sigmoid)
 
@@ -130,5 +132,6 @@ def tile_attend_codepaths_kernel(tc, hid, nodes_words, nodes_scales, s1, s2, s3,
             hi = lo + 128
             nc.scalar.activation(logp[:, lo:hi], prod3[:, lo:hi], ACT.Ln)
             nc.vector.tensor_tensor(res[:, lo:hi], logp[:, lo:hi], pos3[:, lo:hi], ALU.subtract)
-            if hi % 256 == 0:
-                nc.sync.dma_start(out[:, hi - 256 : hi], res[:, hi - 256 : hi])
+            if hi >= 256:
+                first = 0 if hi == 256 else lo
+                nc.sync.dma_start(out[:, first:hi], res[:, first:hi])

from contextlib import ExitStack

import concourse.mybir as mybir

D, T, V, I, Q = 512, 2048, 1024, 512, 128
FLOPS = 2 * D * Q * V

F32 = mybir.dt.float32
BF16 = mybir.dt.bfloat16
I32 = mybir.dt.int32
U32 = mybir.dt.uint32
U16 = mybir.dt.uint16
U8 = mybir.dt.uint8
FP8X4 = mybir.dt.float8_e4m3fn_x4
FP4X4 = mybir.dt.float4_e2m1fn_x4
ALU = mybir.AluOpType
ACT = mybir.ActivationFunctionType

P = 128
PACK = 4
GROUP = 16


def entries(offsets, lo, hi):
    return offsets[:, lo // GROUP : hi // GROUP]


def tile_attend_codepaths_kernel(tc, hid, nodes_words, nodes_scales, s1, s2, s3, offs, offs2, offs3, offs4, out):
    nc = tc.nc
    with ExitStack() as ctx:
        lists = ctx.enter_context(tc.tile_pool(name="lists", bufs=1))
        sb = ctx.enter_context(tc.tile_pool(name="sb", bufs=1))
        psum = ctx.enter_context(tc.psum_pool(name="psum", bufs=1))

        warm_in = sb.tile([P, 1], F32)
        warm_out = sb.tile([P, 1], F32)
        store_scales = sb.tile([P, T], U8, align_bytes=64)
        zero_view = store_scales[:].bitcast(I32)
        nc.vector.memset(zero_view[:, : T // 8], 0)
        nc.gpsimd.memset(zero_view[:, T // 8 :], 0)
        nc.vector.memset(warm_in[:], 0.0)
        nc.scalar.activation(warm_out[:], warm_in[:], ACT.Sigmoid)

        store_words = sb.tile([P, T], U16, align_bytes=64)
        nc.sync.dma_start(store_words[:].bitcast(I32), nodes_words[0].bitcast(I32))
        node_list = lists.tile([P, V // GROUP], U16)
        nc.sync.dma_start(node_list[:], offs)
        hid_raw = sb.tile([P, PACK, Q], F32, tag="rows")
        nc.sync.dma_start(hid_raw[:], hid.rearrange("(p t) q -> p t q", t=PACK))
        for quad in range(4):
            nc.sync.dma_start(
                store_scales[32 * quad : 32 * quad + 4, :].bitcast(I32),
                nodes_scales[0, 4 * quad : 4 * quad + 4, :].bitcast(I32),
            )
        path_lists = []
        for j, offs_j in enumerate((offs2, offs3, offs4)):
            path_list = lists.tile([P, I // GROUP], U16, name="path_list%d" % j)
            nc.sync.dma_start(path_list[:], offs_j)
            path_lists.append(path_list)

        hid_bf = sb.tile([P, Q, PACK], BF16, align_bytes=64, tag="staging")
        nc.scalar.copy(hid_bf[:], hid_raw[:].rearrange("p t q -> p q t"))
        turns = sb.tile([P, 3 * I], F32, tag="rows")
        for j, s_j in enumerate((s1, s2, s3)):
            nc.sync.dma_start(turns[:, j * I : (j + 1) * I], s_j[0].partition_broadcast(P))
        hid_codes = sb.tile([P, Q], U32, align_bytes=64)
        hid_scales = sb.tile([P, Q], U8, align_bytes=64)

        words = sb.tile([P, V], U16, align_bytes=64)
        for lo, hi in ((0, 512), (512, 1024)):
            nc.vector.tensor_copy(words[:, lo:hi], store_words[:].indirect(entries(node_list, lo, hi)))
        nc.vector.quantize_mx(
            out=hid_codes[:].bitcast(FP8X4), scales=hid_scales[:], in_=hid_bf[:].rearrange("p q t -> p (q t)")
        )
        score = sb.tile([P, V], F32, tag="scores")
        scales_a = sb.tile([P, 512], U8, align_bytes=64)
        scales_b = sb.tile([P, 512], U8, align_bytes=64, tag="staging")
        for lo, hi, pieces in ((0, 512, 1), (512, 768, 1), (768, 1024, 2)):
            scales = scales_a if lo < 512 else scales_b
            base = 0 if lo < 512 else 512
            nc.vector.tensor_copy(scales[:, lo - base : hi - base], store_scales[:].indirect(entries(node_list, lo, hi)))
            width = (hi - lo) // pieces
            for piece in range(pieces):
                cols = slice(lo + piece * width, lo + (piece + 1) * width)
                bank = psum.tile([P, width], F32, name="bank%d" % cols.start)
                nc.tensor.matmul_mx(
                    out=bank[:],
                    lhsT=hid_codes[:].bitcast(FP8X4),
                    lhsT_scale=hid_scales[:],
                    rhs=words[:, cols].bitcast(FP4X4),
                    rhs_scale=scales[:, cols.start - base : cols.stop - base],
                    start=True,
                    stop=True,
                )
                if piece == 0:
                    nc.scalar.copy(score[:, cols], bank[:])
                else:
                    nc.vector.tensor_copy(score[:, cols], bank[:])

        x = [sb.tile([P, I], F32, name="x%d" % j) for j in range(3)]
        mag = [sb.tile([P, I], F32, name="mag%d" % j) for j in range(3)]
        sig = [sb.tile([P, I], F32, name="sig%d" % j) for j in range(3)]
        pieces = [(j, lo, lo + w) for j, w in enumerate((256, 256, 128)) for lo in range(0, I, w)]
        waiting = None
        for j, lo, hi in pieces:
            nc.vector.tensor_tensor(
                x[j][:, lo:hi], score[:].indirect(entries(path_lists[j], lo, hi)), turns[:, j * I + lo : j * I + hi], ALU.mult
            )
            nc.scalar.activation(mag[j][:, lo:hi], x[j][:, lo:hi], ACT.Abs)
            if waiting is not None:
                nc.scalar.activation(waiting[0], waiting[1], ACT.Sigmoid)
            waiting = (sig[j][:, lo:hi], mag[j][:, lo:hi])
        nc.scalar.activation(waiting[0], waiting[1], ACT.Sigmoid)

        prod2 = sb.tile([P, I], F32, tag="rows")
        prod3 = sb.tile([P, I], F32)
        pos1 = sb.tile([P, I], F32, tag="scores")
        pos2 = sb.tile([P, I], F32)
        pos3 = sb.tile([P, I], F32)
        logp = sb.tile([P, I], F32)
        res = sb.tile([P, I], F32)
        nc.vector.tensor_scalar(pos1[:], x[0][:], 0.0, None, ALU.max)
        nc.vector.tensor_tensor(prod2[:], sig[0][:], sig[1][:], ALU.mult)
        nc.vector.scalar_tensor_tensor(pos2[:], x[1][:], 0.0, pos1[:], ALU.max, ALU.add)
        for lo in range(0, I, 256):
            cols = slice(lo, lo + 256)
            nc.vector.tensor_tensor(prod3[:, cols], prod2[:, cols], sig[2][:, cols], ALU.mult)
        for lo in range(0, I, 256):
            cols = slice(lo, lo + 256)
            nc.vector.scalar_tensor_tensor(pos3[:, cols], x[2][:, cols], 0.0, pos2[:, cols], ALU.max, ALU.add)
        for lo in range(0, I, 128):
            hi = lo + 128
            nc.scalar.activation(logp[:, lo:hi], prod3[:, lo:hi], ACT.Ln)
            nc.vector.tensor_tensor(res[:, lo:hi], logp[:, lo:hi], pos3[:, lo:hi], ALU.subtract)
            if hi >= 256:
                first = 0 if hi == 256 else lo
                nc.sync.dma_start(out[:, first:hi], res[:, first:hi])
